import numpy as np
import ml_dtypes


def mxq(x, axis, fmt="e4m3"):
    dtype, down = {"e4m3": (ml_dtypes.float8_e4m3fn, 7), "e5m2": (ml_dtypes.float8_e5m2, 14)}[fmt]
    v = np.moveaxis(np.asarray(x, np.float32).astype(ml_dtypes.bfloat16).astype(np.float64), axis, -1)
    blocks = v.reshape(v.shape[:-1] + (-1, 32))
    amax = np.abs(blocks).max(-1, keepdims=True)
    byte = np.maximum(np.where(amax > 0, np.frexp(amax)[1] - 1 + 127, 0) - down, 1)
    scale = np.exp2(byte - 127.0)
    codes = (blocks / scale).astype(np.float32).astype(dtype).astype(np.float64)
    return np.moveaxis((codes * scale).reshape(v.shape), -1, axis)


WIDE = False


def mx_kscale(k):
    if not WIDE:
        return np.ones(k)
    levels = np.array([30, -30])
    if k % 512:
        return np.exp2(np.random.permutation(np.resize(levels, k // 32))).repeat(32)
    a = np.empty((k // 512, 16))
    for p in range(k // 512):
        a[p, :8] = np.random.permutation(np.resize(levels, 8))
        for g in range(8):
            far = levels[np.abs(levels - a[p, g]) >= 10]
            a[p, g + 8] = far[np.random.randint(len(far))]
    return np.exp2(a.ravel()).repeat(32)


def f64(x):
    return np.asarray(x).astype(np.float64)


def striped(idx):
    return np.tile(np.asarray(idx).reshape(-1, 16).T, (8, 1)).astype(np.uint16)


def unstriped(offs):
    return offs[:16].T.reshape(-1).astype(np.int64)


E2M1 = np.array([0.0, 0.5, 1.0, 1.5, 2.0, 3.0, 4.0, 6.0, -0.0, -0.5, -1.0, -1.5, -2.0, -3.0, -4.0, -6.0])


def pack_weight(w, fmt):
    k, n = w.shape
    w = f64(np.asarray(w, np.float32).astype(ml_dtypes.bfloat16)).reshape(k // 32, 32, n)
    amax = np.abs(w).max(1)
    if fmt == "e4m3":
        byte = np.frexp(amax)[1] - 1 + 127 - 7
    else:
        mant, ex = np.frexp(amax / 6.0)
        byte = np.where(mant > 0.5, ex, ex - 1) + 127
    byte = np.clip(np.where(amax > 0, byte, 1), 1, 254)
    scaled = (w * np.exp2(127.0 - byte)[:, None, :]).reshape(k, n).astype(np.float32)
    by_word = np.ascontiguousarray(scaled.reshape(k // 512, 128, 4, n).transpose(0, 1, 3, 2))
    if fmt == "e4m3":
        words = by_word.astype(ml_dtypes.float8_e4m3fn).view(np.uint8)
    else:
        c = by_word.astype(ml_dtypes.float4_e2m1fn).view(np.uint8) & 0xF
        words = (c[..., 0::2] | (c[..., 1::2] << 4)).reshape(k // 512, 128, 2 * n)
    return np.ascontiguousarray(words), np.ascontiguousarray(byte.astype(np.uint8).reshape(k // 512, 16, n))


def unpack_weight(words, scales, fmt):
    g, _, n = scales.shape
    words = np.ascontiguousarray(words).reshape(g, 128, n, -1)
    if fmt == "e4m3":
        vals = words.view(ml_dtypes.float8_e4m3fn).astype(np.float64)
    else:
        nib = np.empty((g, 128, n, 4), np.uint8)
        nib[..., 0::2] = words & 0xF
        nib[..., 1::2] = words >> 4
        vals = E2M1[nib]
    vals = vals * np.repeat(np.exp2(scales.astype(np.float64) - 127.0), 8, axis=1)[..., None]
    return vals.transpose(0, 1, 3, 2).reshape(g * 512, n)


K, T, Z, J, R, O, N, L, E = 512, 1024, 1024, 256, 512, 128, 256, 512, 1024


def setup_inputs():
    n = np.random.standard_normal
    idx = np.random.permutation(T)[:J]
    idx2 = np.random.permutation(Z)[:J]
    idx3 = np.random.permutation(J)[:O]
    idx4 = np.random.permutation(J)[:O]
    idx5 = np.random.permutation(E)[:O]
    fk = mx_kscale(K)
    fr = mx_kscale(R)
    fl = mx_kscale(L)
    xtp = pack_weight(n((K, T)) / fk[:, None], "e2m1")
    xop = pack_weight(n((K, Z)) / fk[:, None], "e4m3")
    wp = pack_weight(n((K, R)) * 1 / np.sqrt(K) * fk[:, None] * fr, "e4m3")
    wbp = pack_weight(n((R, N)) * 1 / np.sqrt(R) / fr[:, None], "e2m1")
    sxp = pack_weight(n((L, O)) / fl[:, None], "e4m3")
    wsp = pack_weight(n((L, N)) * 1 / np.sqrt(L) * fl[:, None], "e4m3")
    return {
        "xt_words": xtp[0],
        "xt_scales": xtp[1],
        "xo_words": xop[0],
        "xo_scales": xop[1],
        "w_words": wp[0],
        "w_scales": wp[1],
        "wb_words": wbp[0],
        "wb_scales": wbp[1],
        "sx_words": sxp[0],
        "sx_scales": sxp[1],
        "ws_words": wsp[0],
        "ws_scales": wsp[1],
        "offs": striped(idx),
        "offs2": striped(idx2),
        "offs3": striped(idx3),
        "offs4": striped(idx4),
        "offs5": striped(idx5),
    }


def reference(xt_words, xt_scales, xo_words, xo_scales, w_words, w_scales, wb_words, wb_scales, sx_words, sx_scales, ws_words, ws_scales, offs, offs2, offs3, offs4, offs5):
    idx = unstriped(offs)
    idx2 = unstriped(offs2)
    idx3 = unstriped(offs3)
    idx4 = unstriped(offs4)
    idx5 = unstriped(offs5)
    xtu = unpack_weight(xt_words, xt_scales, "e2m1")
    xou = unpack_weight(xo_words, xo_scales, "e4m3")
    wu = unpack_weight(w_words, w_scales, "e4m3")
    wbu = unpack_weight(wb_words, wb_scales, "e2m1")
    sxu = unpack_weight(sx_words, sx_scales, "e4m3")
    wsu = unpack_weight(ws_words, ws_scales, "e4m3")
    xtidxg = xtu[:, idx]
    a = wu.T @ xtidxg
    xoidx2g = xou[:, idx2]
    b = wu.T @ xoidx2g
    hid = np.maximum(a[:, idx3], b[:, idx4])
    hidq = mxq(hid, 0, "e5m2")
    p = wbu.T @ hidq + wsu.T @ sxu
    y = np.zeros((N, E))
    y[:, idx5] = p
    return y

@@ -1,0 +1,171 @@
+from contextlib import ExitStack
+
+import concourse.mybir as mybir
+
+FLOPS = 335544320
+
+F32 = mybir.dt.float32
+BF16 = mybir.dt.bfloat16
+I32 = mybir.dt.int32
+U32 = mybir.dt.uint32
+U16 = mybir.dt.uint16
+U8 = mybir.dt.uint8
+E4M3 = mybir.dt.float8_e4m3fn_x4
+E5M2 = mybir.dt.float8_e5m2_x4
+E2M1 = mybir.dt.float4_e2m1fn_x4
+COPY = mybir.ActivationFunctionType.Copy
+MAX = mybir.AluOpType.max
+
+P = 128
+T, J, R, O, N, E = 1024, 256, 512, 128, 256, 1024
+
+
+def load_scale_quadrant(queue, plane, rows, q):
+    queue.dma_start(out=plane[32 * q : 32 * q + 4, :].bitcast(I32), in_=rows[0, 4 * q : 4 * q + 4, :].bitcast(I32))
+
+
+def load_scale_rows(queue, plane, rows, quadrants=range(4)):
+    for q in quadrants:
+        load_scale_quadrant(queue, plane, rows, q)
+
+
+def words_of(packed):
+    return packed[0].rearrange("p c t -> p (c t)").bitcast(I32)
+
+
+def tile_list_oneforboth_looked_skip_scattered_kernel(
+    tc, xt_words, xt_scales, xo_words, xo_scales, w_words, w_scales, wb_words, wb_scales,
+    sx_words, sx_scales, ws_words, ws_scales, offs, offs2, offs3, offs4, offs5, out,
+):
+    nc = tc.nc
+    with ExitStack() as ctx:
+        sb = ctx.enter_context(tc.tile_pool(name="sb", bufs=1))
+        ps = ctx.enter_context(tc.psum_pool(name="ps", bufs=1))
+
+        l1 = sb.tile([P, J // 16], U16, name="l1")
+        l2 = sb.tile([P, J // 16], U16, name="l2")
+        l3 = sb.tile([P, O // 16], U16, name="l3")
+        l4 = sb.tile([P, O // 16], U16, name="l4")
+        l5 = sb.tile([P, O // 16], U16, name="l5")
+        xt_w = sb.tile([P, T], U16, name="xt_w", align_bytes=64)
+        xt_s = sb.tile([P, T], U8, name="xt_s", align_bytes=64)
+        xo_w = sb.tile([P, T], U32, name="xo_w", align_bytes=64)
+        xo_s = sb.tile([P, T], U8, name="xo_s", align_bytes=64)
+        w_w = sb.tile([P, R], U32, name="w_w", align_bytes=64)
+        w_s = sb.tile([P, R], U8, name="w_s", align_bytes=64)
+        wb_w = sb.tile([P, 2 * N], U8, name="wb_w", align_bytes=64)
+        ws_w = sb.tile([P, N], U32, name="ws_w", align_bytes=64)
+        sx_w = sb.tile([P, O], U32, name="sx_w", align_bytes=64)
+        late_s = sb.tile([P, 2 * N + O], U8, name="late_s", align_bytes=64)
+        wb_s = late_s[:, 0:N]
+        ws_s = late_s[:, N : 2 * N]
+        sx_s = late_s[:, 2 * N : 2 * N + O]
+        pages = [sb.tile([P, E], F32, name="page%d" % h) for h in range(2)]
+
+        nc.vector.memset(xt_s[:].bitcast(I32), 0)
+        nc.vector.memset(w_s[:].bitcast(I32), 0)
+        nc.vector.memset(xo_s[:].bitcast(I32), 0)
+        nc.vector.memset(late_s[:].bitcast(I32), 0)
+        for h in range(2):
+            nc.vector.memset(pages[h][:], 0.0)
+
+        nc.sync.dma_start(l1[:], offs)
+        nc.sync.dma_start(out=xt_w[:].bitcast(I32), in_=xt_words[0].bitcast(I32))
+        load_scale_rows(nc.scalar, xt_s, xt_scales)
+        nc.sync.dma_start(out=w_w[:].bitcast(I32), in_=words_of(w_words))
+        nc.sync.dma_start(out=xo_w[:].bitcast(I32), in_=words_of(xo_words))
+        load_scale_rows(nc.sync, w_s, w_scales)
+        nc.sync.dma_start(l2[:], offs2)
+        load_scale_rows(nc.sync, xo_s, xo_scales)
+        nc.sync.dma_start(l3[:], offs3)
+        nc.sync.dma_start(l4[:], offs4)
+        nc.sync.dma_start(out=ws_w[:].bitcast(I32), in_=words_of(ws_words))
+        nc.sync.dma_start(out=sx_w[:].bitcast(I32), in_=words_of(sx_words))
+        load_scale_rows(nc.sync, ws_s, ws_scales)
+        load_scale_rows(nc.sync, sx_s, sx_scales)
+        nc.sync.dma_start(out=wb_w[:].bitcast(I32), in_=wb_words[0].bitcast(I32))
+        load_scale_rows(nc.sync, wb_s, wb_scales)
+        nc.sync.dma_start(l5[:], offs5)
+
+        xtg_w = sb.tile([P, J], U16, name="xtg_w", align_bytes=64)
+        xtg_s = sb.tile([P, J], U8, name="xtg_s", align_bytes=64)
+        xog_w = sb.tile([P, J], U32, name="xog_w", align_bytes=64)
+        xog_s = sb.tile([P, J], U8, name="xog_s", align_bytes=64)
+        wd_w = sb.tile([P, 4, P], U32, name="wd_w", align_bytes=64)
+        wd_s = sb.tile([P, 4, P], U8, name="wd_s", align_bytes=64)
+
+        nc.vector.tensor_copy(xtg_w[:], xt_w[:].indirect(l1[:]))
+        nc.vector.tensor_copy(xtg_s[:], xt_s[:].indirect(l1[:]))
+        nc.scalar.copy(out=wd_w[:], in_=w_w[:].rearrange("p (q t) -> p t q", t=4))
+        nc.vector.tensor_copy(out=wd_s[:], in_=w_s[:].rearrange("p (q t) -> p t q", t=4))
+        nc.vector.tensor_copy(xog_w[:], xo_w[:].indirect(l2[:]))
+        nc.vector.tensor_copy(xog_s[:], xo_s[:].indirect(l2[:]))
+
+        a_ps = [ps.tile([P, 2, J], F32, name="a_ps%d" % u) for u in range(2)]
+        b_ps = [ps.tile([P, 2, J], F32, name="b_ps%d" % u) for u in range(2)]
+        for bank, words, scales in ((a_ps, xtg_w[:].bitcast(E2M1), xtg_s), (b_ps, xog_w[:].bitcast(E4M3), xog_s)):
+            for t in range(4):
+                nc.tensor.matmul_mx(
+                    out=bank[t // 2][:, t % 2, :], lhsT=wd_w[:, t, :].bitcast(E4M3), lhsT_scale=wd_s[:, t, :],
+                    rhs=words, rhs_scale=scales[:], start=True, stop=True,
+                )
+
+        p_ps = [ps.tile([P, O], F32, name="p_ps%d" % h) for h in range(2)]
+        for h in range(2):
+            nc.tensor.matmul_mx(
+                out=p_ps[h][:], lhsT=ws_w[:, P * h : P * (h + 1)].bitcast(E4M3), lhsT_scale=ws_s[:, P * h : P * (h + 1)],
+                rhs=sx_w[:].bitcast(E4M3), rhs_scale=sx_s, start=True, stop=False,
+            )
+
+        a_sb = [sb.tile([P, 2, J], F32, name="a_sb%d" % u) for u in range(2)]
+        b_sb = [sb.tile([P, 2, J], F32, name="b_sb%d" % u) for u in range(2)]
+        ga = sb.tile([P, 4, O], F32, name="ga")
+        gb = sb.tile([P, 4, O], F32, name="gb")
+
+        def pick_v(dst, src, lst, t):
+            nc.vector.tensor_copy(dst[:, t, :], src[t // 2][:, t % 2, :].indirect(lst[:]))
+
+        def pick_s(dst, src, lst, t):
+            nc.scalar.activation(dst[:, t, :], src[t // 2][:, t % 2, :].indirect(lst[:]), COPY)
+
+        hid = sb.tile([P, O, 4], BF16, name="hid", align_bytes=64)
+
+        def larger(u):
+            nc.vector.tensor_tensor(
+                out=hid[:, :, 2 * u : 2 * u + 2],
+                in0=ga[:, 2 * u : 2 * u + 2, :].rearrange("p t o -> p o t"),
+                in1=gb[:, 2 * u : 2 * u + 2, :].rearrange("p t o -> p o t"),
+                op=MAX,
+            )
+
+        nc.scalar.activation(a_sb[0][:], a_ps[0][:], COPY)
+        nc.scalar.activation(a_sb[1][:], a_ps[1][:], COPY)
+        pick_v(ga, a_sb, l3, 0)
+        pick_v(ga, a_sb, l3, 1)
+        pick_s(ga, a_sb, l3, 2)
+        pick_s(ga, a_sb, l3, 3)
+        nc.vector.tensor_copy(b_sb[0][:], b_ps[0][:])
+        nc.scalar.activation(b_sb[1][:], b_ps[1][:], COPY)
+        pick_v(gb, b_sb, l4, 0)
+        pick_v(gb, b_sb, l4, 1)
+        pick_s(gb, b_sb, l4, 2)
+        pick_s(gb, b_sb, l4, 3)
+        larger(0)
+        larger(1)
+        hq_w = sb.tile([P, O], U32, name="hq_w", align_bytes=64)
+        hq_s = sb.tile([P, O], U8, name="hq_s", align_bytes=64)
+        nc.vector.quantize_mx(out=hq_w[:].bitcast(E5M2), scales=hq_s[:], in_=hid[:].rearrange("p o t -> p (o t)"))
+
+        for h in range(2):
+            nc.tensor.matmul_mx(
+                out=p_ps[h][:], lhsT=wb_w[:, 2 * P * h : 2 * P * (h + 1)].bitcast(E2M1), lhsT_scale=wb_s[:, P * h : P * (h + 1)],
+                rhs=hq_w[:].bitcast(E5M2), rhs_scale=hq_s[:], start=False, stop=True,
+            )
+
+        p_sb = [sb.tile([P, O], F32, name="p_sb%d" % h) for h in range(2)]
+        nc.vector.tensor_copy(p_sb[0][:], p_ps[0][:])
+        nc.vector.tensor_copy(pages[0][:].indirect(l5[:]), p_sb[0][:])
+        nc.sync.dma_start(out=out[0:P, :], in_=pages[0][:])
+        nc.scalar.activation(p_sb[1][:], p_ps[1][:], COPY)
+        nc.scalar.activation(pages[1][:].indirect(l5[:]), p_sb[1][:], COPY)
+        nc.scalar.dma_start(out=out[P : 2 * P, :], in_=pages[1][:])

@@ -70,12 +70,12 @@ def tile_list_oneforboth_looked_skip_scattered_kernel(
             nc.vector.memset(pages[h][:], 0.0)
 
         nc.sync.dma_start(l1[:], offs)
-        nc.sync.dma_start(out=xt_w[:].bitcast(I32), in_=xt_words[0].bitcast(I32))
-        load_scale_rows(nc.scalar, xt_s, xt_scales)
-        nc.sync.dma_start(out=w_w[:].bitcast(I32), in_=words_of(w_words))
-        nc.sync.dma_start(out=xo_w[:].bitcast(I32), in_=words_of(xo_words))
-        load_scale_rows(nc.sync, w_s, w_scales)
         nc.sync.dma_start(l2[:], offs2)
+        load_scale_rows(nc.sync, xt_s, xt_scales)
+        nc.sync.dma_start(out=xt_w[:].bitcast(I32), in_=xt_words[0].bitcast(I32))
+        nc.sync.dma_start(out=w_w[:].bitcast(I32), in_=words_of(w_words))
+        load_scale_rows(nc.sync, w_s, w_scales)
+        nc.sync.dma_start(out=xo_w[:].bitcast(I32), in_=words_of(xo_words))
         load_scale_rows(nc.sync, xo_s, xo_scales)
         nc.sync.dma_start(l3[:], offs3)
         nc.sync.dma_start(l4[:], offs4)
@@ -91,22 +91,26 @@ def tile_list_oneforboth_looked_skip_scattered_kernel(
         xtg_s = sb.tile([P, J], U8, name="xtg_s", align_bytes=64)
         xog_w = sb.tile([P, J], U32, name="xog_w", align_bytes=64)
         xog_s = sb.tile([P, J], U8, name="xog_s", align_bytes=64)
-        wd_w = sb.tile([P, 4, P], U32, name="wd_w", align_bytes=64)
-        wd_s = sb.tile([P, 4, P], U8, name="wd_s", align_bytes=64)
+        wd_w = [sb.tile([P, 2, P], U32, name="wd_w%d" % u, align_bytes=64) for u in range(2)]
+        wd_s = [sb.tile([P, 2, P], U8, name="wd_s%d" % u, align_bytes=64) for u in range(2)]
 
-        nc.vector.tensor_copy(xtg_w[:], xt_w[:].indirect(l1[:]))
         nc.vector.tensor_copy(xtg_s[:], xt_s[:].indirect(l1[:]))
-        nc.scalar.copy(out=wd_w[:], in_=w_w[:].rearrange("p (q t) -> p t q", t=4))
-        nc.vector.tensor_copy(out=wd_s[:], in_=w_s[:].rearrange("p (q t) -> p t q", t=4))
+        nc.vector.tensor_copy(xtg_w[:], xt_w[:].indirect(l1[:]))
+        for u in range(2):
+            pair = slice(2 * u, 2 * u + 2)
+            nc.scalar.copy(out=wd_w[u][:], in_=w_w[:].rearrange("p (q t) -> p t q", t=4)[:, pair, :])
+            nc.vector.tensor_copy(out=wd_s[u][:], in_=w_s[:].rearrange("p (q t) -> p t q", t=4)[:, pair, :])
         nc.vector.tensor_copy(xog_w[:], xo_w[:].indirect(l2[:]))
         nc.vector.tensor_copy(xog_s[:], xo_s[:].indirect(l2[:]))
 
         a_ps = [ps.tile([P, 2, J], F32, name="a_ps%d" % u) for u in range(2)]
-        b_ps = [ps.tile([P, 2, J], F32, name="b_ps%d" % u) for u in range(2)]
-        for bank, words, scales in ((a_ps, xtg_w[:].bitcast(E2M1), xtg_s), (b_ps, xog_w[:].bitcast(E4M3), xog_s)):
+        b_ps = [ps.tile([P, J], F32, name="b_ps%d" % t) for t in range(4)]
+        a_out = [a_ps[t // 2][:, t % 2, :] for t in range(4)]
+        b_out = [b_ps[t][:] for t in range(4)]
+        for bank, words, scales in ((a_out, xtg_w[:].bitcast(E2M1), xtg_s), (b_out, xog_w[:].bitcast(E4M3), xog_s)):
             for t in range(4):
                 nc.tensor.matmul_mx(
-                    out=bank[t // 2][:, t % 2, :], lhsT=wd_w[:, t, :].bitcast(E4M3), lhsT_scale=wd_s[:, t, :],
+                    out=bank[t], lhsT=wd_w[t // 2][:, t % 2, :].bitcast(E4M3), lhsT_scale=wd_s[t // 2][:, t % 2, :],
                     rhs=words, rhs_scale=scales[:], start=True, stop=True,
                 )
 
@@ -144,8 +148,10 @@ def tile_list_oneforboth_looked_skip_scattered_kernel(
         pick_v(ga, a_sb, l3, 1)
         pick_s(ga, a_sb, l3, 2)
         pick_s(ga, a_sb, l3, 3)
-        nc.vector.tensor_copy(b_sb[0][:], b_ps[0][:])
-        nc.scalar.activation(b_sb[1][:], b_ps[1][:], COPY)
+        for t in range(2):
+            nc.vector.tensor_copy(b_sb[0][:, t, :], b_ps[t][:])
+        for t in range(2):
+            nc.scalar.activation(b_sb[1][:, t, :], b_ps[2 + t][:], COPY)
         pick_v(gb, b_sb, l4, 0)
         pick_v(gb, b_sb, l4, 1)
         pick_s(gb, b_sb, l4, 2)

@@ -20,8 +20,8 @@ P = 128
 T, J, R, O, N, E = 1024, 256, 512, 128, 256, 1024
 
 
-def load_scale_quadrant(queue, plane, rows, q):
-    queue.dma_start(out=plane[32 * q : 32 * q + 4, :].bitcast(I32), in_=rows[0, 4 * q : 4 * q + 4, :].bitcast(I32))
+def load_scale_quadrant(queue, plane, rows, r):
+    queue.dma_start(out=plane[r:P:32, :].bitcast(I32), in_=rows[0, r:16:4, :].bitcast(I32))
 
 
 def load_scale_rows(queue, plane, rows, quadrants=range(4)):
@@ -78,9 +78,9 @@ def tile_list_oneforboth_looked_skip_scattered_kernel(
         nc.sync.dma_start(out=xo_w[:].bitcast(I32), in_=words_of(xo_words))
         load_scale_rows(nc.sync, xo_s, xo_scales)
         nc.sync.dma_start(l3[:], offs3)
-        nc.sync.dma_start(l4[:], offs4)
         nc.sync.dma_start(out=ws_w[:].bitcast(I32), in_=words_of(ws_words))
         nc.sync.dma_start(out=sx_w[:].bitcast(I32), in_=words_of(sx_words))
+        nc.sync.dma_start(l4[:], offs4)
         load_scale_rows(nc.sync, ws_s, ws_scales)
         load_scale_rows(nc.sync, sx_s, sx_scales)
         nc.sync.dma_start(out=wb_w[:].bitcast(I32), in_=wb_words[0].bitcast(I32))
@@ -90,7 +90,7 @@ def tile_list_oneforboth_looked_skip_scattered_kernel(
         xtg_w = sb.tile([P, J], U16, name="xtg_w", align_bytes=64)
         xtg_s = sb.tile([P, J], U8, name="xtg_s", align_bytes=64)
         xog_w = sb.tile([P, J], U32, name="xog_w", align_bytes=64)
-        xog_s = sb.tile([P, J], U8, name="xog_s", align_bytes=64)
+        xog_s = [sb.tile([P, P], U8, name="xog_s%d" % g, align_bytes=64) for g in range(2)]
         wd_w = [sb.tile([P, 2, P], U32, name="wd_w%d" % u, align_bytes=64) for u in range(2)]
         wd_s = [sb.tile([P, 2, P], U8, name="wd_s%d" % u, align_bytes=64) for u in range(2)]
 
@@ -98,21 +98,26 @@ def tile_list_oneforboth_looked_skip_scattered_kernel(
         nc.vector.tensor_copy(xtg_w[:], xt_w[:].indirect(l1[:]))
         for u in range(2):
             pair = slice(2 * u, 2 * u + 2)
-            nc.scalar.copy(out=wd_w[u][:], in_=w_w[:].rearrange("p (q t) -> p t q", t=4)[:, pair, :])
+            nc.scalar.copy(out=wd_w[u][:].rearrange("p t q -> p q t"), in_=w_w[:].rearrange("p (q t) -> p q t", t=4)[:, :, pair])
             nc.vector.tensor_copy(out=wd_s[u][:], in_=w_s[:].rearrange("p (q t) -> p t q", t=4)[:, pair, :])
         nc.vector.tensor_copy(xog_w[:], xo_w[:].indirect(l2[:]))
-        nc.vector.tensor_copy(xog_s[:], xo_s[:].indirect(l2[:]))
+        for g in range(2):
+            nc.vector.tensor_copy(xog_s[g][:], xo_s[:].indirect(l2[:, 8 * g : 8 * g + 8]))
 
         a_ps = [ps.tile([P, 2, J], F32, name="a_ps%d" % u) for u in range(2)]
         b_ps = [ps.tile([P, J], F32, name="b_ps%d" % t) for t in range(4)]
-        a_out = [a_ps[t // 2][:, t % 2, :] for t in range(4)]
-        b_out = [b_ps[t][:] for t in range(4)]
-        for bank, words, scales in ((a_out, xtg_w[:].bitcast(E2M1), xtg_s), (b_out, xog_w[:].bitcast(E4M3), xog_s)):
+        def first_stage(dst, t, words, scales):
+            nc.tensor.matmul_mx(
+                out=dst, lhsT=wd_w[t // 2][:, t % 2, :].bitcast(E4M3), lhsT_scale=wd_s[t // 2][:, t % 2, :],
+                rhs=words, rhs_scale=scales, start=True, stop=True,
+            )
+
+        for t in range(4):
+            first_stage(a_ps[t // 2][:, t % 2, :], t, xtg_w[:].bitcast(E2M1), xtg_s[:])
+        for g in range(2):
+            cols = slice(P * g, P * (g + 1))
             for t in range(4):
-                nc.tensor.matmul_mx(
-                    out=bank[t], lhsT=wd_w[t // 2][:, t % 2, :].bitcast(E4M3), lhsT_scale=wd_s[t // 2][:, t % 2, :],
-                    rhs=words, rhs_scale=scales[:], start=True, stop=True,
-                )
+                first_stage(b_ps[t][:, cols], t, xog_w[:, cols].bitcast(E4M3), xog_s[g][:])
 
         p_ps = [ps.tile([P, O], F32, name="p_ps%d" % h) for h in range(2)]
         for h in range(2):
@@ -148,14 +153,12 @@ def tile_list_oneforboth_looked_skip_scattered_kernel(
         pick_v(ga, a_sb, l3, 1)
         pick_s(ga, a_sb, l3, 2)
         pick_s(ga, a_sb, l3, 3)
-        for t in range(2):
-            nc.vector.tensor_copy(b_sb[0][:, t, :], b_ps[t][:])
-        for t in range(2):
-            nc.scalar.activation(b_sb[1][:, t, :], b_ps[2 + t][:], COPY)
-        pick_v(gb, b_sb, l4, 0)
-        pick_v(gb, b_sb, l4, 1)
-        pick_s(gb, b_sb, l4, 2)
-        pick_s(gb, b_sb, l4, 3)
+        for u in range(2):
+            nc.vector.tensor_copy(b_sb[u][:, 0, :], b_ps[2 * u][:])
+            nc.scalar.activation(b_sb[u][:, 1, :], b_ps[2 * u + 1][:], COPY)
+        for u in range(2):
+            pick_v(gb, b_sb, l4, 2 * u)
+            pick_s(gb, b_sb, l4, 2 * u + 1)
         larger(0)
         larger(1)
         hq_w = sb.tile([P, O], U32, name="hq_w", align_bytes=64)

@@ -17,20 +17,33 @@ COPY = mybir.ActivationFunctionType.Copy
 MAX = mybir.AluOpType.max
 
 P = 128
-T, J, R, O, N, E = 1024, 256, 512, 128, 256, 1024
+PACK = 4
+QUADRANT = 32
+BLOCKS = 16
+LIST_ROWS = 16
+T = 1024
+J = 256
+R = 512
+O = 128
+N = 256
+E = 1024
+HALVES = range(2)
 
 
-def load_scale_quadrant(queue, plane, rows, r):
-    queue.dma_start(out=plane[r:P:32, :].bitcast(I32), in_=rows[0, r:16:4, :].bitcast(I32))
+def load_scale_rows(nc, scale_tile, rows):
+    per_quadrant = BLOCKS * QUADRANT // P
+    for i in range(per_quadrant):
+        nc.sync.dma_start(
+            out=scale_tile[i:P:QUADRANT, :].bitcast(I32), in_=rows[0, i:BLOCKS:per_quadrant, :].bitcast(I32)
+        )
 
 
-def load_scale_rows(queue, plane, rows, quadrants=range(4)):
-    for q in quadrants:
-        load_scale_quadrant(queue, plane, rows, q)
+def load_bytes(nc, tile, packed):
+    nc.sync.dma_start(out=tile[:].bitcast(I32), in_=packed.bitcast(I32))
 
 
-def words_of(packed):
-    return packed[0].rearrange("p c t -> p (c t)").bitcast(I32)
+def e4m3_rows(words):
+    return words[0].rearrange("p c t -> p (c t)")
 
 
 def tile_list_oneforboth_looked_skip_scattered_kernel(
@@ -42,11 +55,11 @@ def tile_list_oneforboth_looked_skip_scattered_kernel(
         sb = ctx.enter_context(tc.tile_pool(name="sb", bufs=1))
         ps = ctx.enter_context(tc.psum_pool(name="ps", bufs=1))
 
-        l1 = sb.tile([P, J // 16], U16, name="l1")
-        l2 = sb.tile([P, J // 16], U16, name="l2")
-        l3 = sb.tile([P, O // 16], U16, name="l3")
-        l4 = sb.tile([P, O // 16], U16, name="l4")
-        l5 = sb.tile([P, O // 16], U16, name="l5")
+        idx = sb.tile([P, J // LIST_ROWS], U16, name="idx")
+        idx2 = sb.tile([P, J // LIST_ROWS], U16, name="idx2")
+        idx3 = sb.tile([P, O // LIST_ROWS], U16, name="idx3")
+        idx4 = sb.tile([P, O // LIST_ROWS], U16, name="idx4")
+        idx5 = sb.tile([P, O // LIST_ROWS], U16, name="idx5")
         xt_w = sb.tile([P, T], U16, name="xt_w", align_bytes=64)
         xt_s = sb.tile([P, T], U8, name="xt_s", align_bytes=64)
         xo_w = sb.tile([P, T], U32, name="xo_w", align_bytes=64)
@@ -56,125 +69,133 @@ def tile_list_oneforboth_looked_skip_scattered_kernel(
         wb_w = sb.tile([P, 2 * N], U8, name="wb_w", align_bytes=64)
         ws_w = sb.tile([P, N], U32, name="ws_w", align_bytes=64)
         sx_w = sb.tile([P, O], U32, name="sx_w", align_bytes=64)
-        late_s = sb.tile([P, 2 * N + O], U8, name="late_s", align_bytes=64)
-        wb_s = late_s[:, 0:N]
-        ws_s = late_s[:, N : 2 * N]
-        sx_s = late_s[:, 2 * N : 2 * N + O]
-        pages = [sb.tile([P, E], F32, name="page%d" % h) for h in range(2)]
+        stage2_s = sb.tile([P, 2 * N + O], U8, name="stage2_s", align_bytes=64)
+        wb_s = stage2_s[:, 0:N]
+        ws_s = stage2_s[:, N : 2 * N]
+        sx_s = stage2_s[:, 2 * N : 2 * N + O]
+        pages = [sb.tile([P, E], F32, name="page%d" % h) for h in HALVES]
 
-        nc.vector.memset(xt_s[:].bitcast(I32), 0)
-        nc.vector.memset(w_s[:].bitcast(I32), 0)
-        nc.vector.memset(xo_s[:].bitcast(I32), 0)
-        nc.vector.memset(late_s[:].bitcast(I32), 0)
-        for h in range(2):
+        for scale_tile in (xt_s, w_s, xo_s, stage2_s):
+            nc.vector.memset(scale_tile[:].bitcast(I32), 0)
+        for h in HALVES:
             nc.vector.memset(pages[h][:], 0.0)
 
-        nc.sync.dma_start(l1[:], offs)
-        nc.sync.dma_start(l2[:], offs2)
-        load_scale_rows(nc.sync, xt_s, xt_scales)
-        nc.sync.dma_start(out=xt_w[:].bitcast(I32), in_=xt_words[0].bitcast(I32))
-        nc.sync.dma_start(out=w_w[:].bitcast(I32), in_=words_of(w_words))
-        load_scale_rows(nc.sync, w_s, w_scales)
-        nc.sync.dma_start(out=xo_w[:].bitcast(I32), in_=words_of(xo_words))
-        load_scale_rows(nc.sync, xo_s, xo_scales)
-        nc.sync.dma_start(l3[:], offs3)
-        nc.sync.dma_start(out=ws_w[:].bitcast(I32), in_=words_of(ws_words))
-        nc.sync.dma_start(out=sx_w[:].bitcast(I32), in_=words_of(sx_words))
-        nc.sync.dma_start(l4[:], offs4)
-        load_scale_rows(nc.sync, ws_s, ws_scales)
-        load_scale_rows(nc.sync, sx_s, sx_scales)
-        nc.sync.dma_start(out=wb_w[:].bitcast(I32), in_=wb_words[0].bitcast(I32))
-        load_scale_rows(nc.sync, wb_s, wb_scales)
-        nc.sync.dma_start(l5[:], offs5)
+        nc.sync.dma_start(idx[:], offs)
+        nc.sync.dma_start(idx2[:], offs2)
+        load_scale_rows(nc, xt_s, xt_scales)
+        load_bytes(nc, xt_w, xt_words[0])
+        load_bytes(nc, w_w, e4m3_rows(w_words))
+        load_scale_rows(nc, w_s, w_scales)
+        load_bytes(nc, xo_w, e4m3_rows(xo_words))
+        load_scale_rows(nc, xo_s, xo_scales)
+        nc.sync.dma_start(idx3[:], offs3)
+        load_bytes(nc, ws_w, e4m3_rows(ws_words))
+        load_bytes(nc, sx_w, e4m3_rows(sx_words))
+        nc.sync.dma_start(idx4[:], offs4)
+        load_scale_rows(nc, ws_s, ws_scales)
+        load_scale_rows(nc, sx_s, sx_scales)
+        load_bytes(nc, wb_w, wb_words[0])
+        load_scale_rows(nc, wb_s, wb_scales)
+        nc.sync.dma_start(idx5[:], offs5)
 
-        xtg_w = sb.tile([P, J], U16, name="xtg_w", align_bytes=64)
-        xtg_s = sb.tile([P, J], U8, name="xtg_s", align_bytes=64)
-        xog_w = sb.tile([P, J], U32, name="xog_w", align_bytes=64)
-        xog_s = [sb.tile([P, P], U8, name="xog_s%d" % g, align_bytes=64) for g in range(2)]
-        wd_w = [sb.tile([P, 2, P], U32, name="wd_w%d" % u, align_bytes=64) for u in range(2)]
-        wd_s = [sb.tile([P, 2, P], U8, name="wd_s%d" % u, align_bytes=64) for u in range(2)]
+        xt_picked_w = sb.tile([P, J], U16, name="xt_picked_w", align_bytes=64)
+        xt_picked_s = sb.tile([P, J], U8, name="xt_picked_s", align_bytes=64)
+        xo_picked_w = sb.tile([P, J], U32, name="xo_picked_w", align_bytes=64)
+        xo_picked_s = sb.tile([P, J], U8, name="xo_picked_s", align_bytes=64)
+        dealt_w = [sb.tile([P, 2, P], U32, name="dealt_w%d" % u, align_bytes=64) for u in HALVES]
+        dealt_s = [sb.tile([P, 2, P], U8, name="dealt_s%d" % u, align_bytes=64) for u in HALVES]
 
-        nc.vector.tensor_copy(xtg_s[:], xt_s[:].indirect(l1[:]))
-        nc.vector.tensor_copy(xtg_w[:], xt_w[:].indirect(l1[:]))
-        for u in range(2):
+        nc.vector.tensor_copy(xt_picked_s[:], xt_s[:].indirect(idx[:]))
+        nc.vector.tensor_copy(xt_picked_w[:], xt_w[:].indirect(idx[:]))
+        for u in HALVES:
             pair = slice(2 * u, 2 * u + 2)
-            nc.scalar.copy(out=wd_w[u][:].rearrange("p t q -> p q t"), in_=w_w[:].rearrange("p (q t) -> p q t", t=4)[:, :, pair])
-            nc.vector.tensor_copy(out=wd_s[u][:], in_=w_s[:].rearrange("p (q t) -> p t q", t=4)[:, pair, :])
-        nc.vector.tensor_copy(xog_w[:], xo_w[:].indirect(l2[:]))
-        for g in range(2):
-            nc.vector.tensor_copy(xog_s[g][:], xo_s[:].indirect(l2[:, 8 * g : 8 * g + 8]))
+            nc.scalar.copy(
+                out=dealt_w[u][:].rearrange("p t q -> p q t"),
+                in_=w_w[:].rearrange("p (q t) -> p q t", t=PACK)[:, :, pair],
+            )
+            nc.vector.tensor_copy(out=dealt_s[u][:], in_=w_s[:].rearrange("p (q t) -> p t q", t=PACK)[:, pair, :])
+        nc.vector.tensor_copy(xo_picked_w[:], xo_w[:].indirect(idx2[:]))
+        half_list = P // LIST_ROWS
+        for g in HALVES:
+            nc.vector.tensor_copy(
+                xo_picked_s[:, P * g : P * (g + 1)], xo_s[:].indirect(idx2[:, half_list * g : half_list * (g + 1)])
+            )
 
-        a_ps = [ps.tile([P, 2, J], F32, name="a_ps%d" % u) for u in range(2)]
-        b_ps = [ps.tile([P, J], F32, name="b_ps%d" % t) for t in range(4)]
+        a_ps = [ps.tile([P, 2, J], F32, name="a_ps%d" % u) for u in HALVES]
+        b_ps = [ps.tile([P, J], F32, name="b_ps%d" % t) for t in range(PACK)]
+
         def first_stage(dst, t, words, scales):
             nc.tensor.matmul_mx(
-                out=dst, lhsT=wd_w[t // 2][:, t % 2, :].bitcast(E4M3), lhsT_scale=wd_s[t // 2][:, t % 2, :],
+                out=dst, lhsT=dealt_w[t // 2][:, t % 2, :].bitcast(E4M3), lhsT_scale=dealt_s[t // 2][:, t % 2, :],
                 rhs=words, rhs_scale=scales, start=True, stop=True,
             )
 
-        for t in range(4):
-            first_stage(a_ps[t // 2][:, t % 2, :], t, xtg_w[:].bitcast(E2M1), xtg_s[:])
-        for g in range(2):
-            cols = slice(P * g, P * (g + 1))
-            for t in range(4):
-                first_stage(b_ps[t][:, cols], t, xog_w[:, cols].bitcast(E4M3), xog_s[g][:])
+        for t in range(PACK):
+            first_stage(a_ps[t // 2][:, t % 2, :], t, xt_picked_w[:].bitcast(E2M1), xt_picked_s[:])
+        for g in HALVES:
+            slots = slice(P * g, P * (g + 1))
+            for t in range(2):
+                first_stage(b_ps[t][:, slots], t, xo_picked_w[:, slots].bitcast(E4M3), xo_picked_s[:, slots])
+        for t in range(2, PACK):
+            first_stage(b_ps[t][:], t, xo_picked_w[:].bitcast(E4M3), xo_picked_s[:])
 
-        p_ps = [ps.tile([P, O], F32, name="p_ps%d" % h) for h in range(2)]
-        for h in range(2):
+        p_ps = [ps.tile([P, O], F32, name="p_ps%d" % h) for h in HALVES]
+        for h in HALVES:
+            features = slice(P * h, P * (h + 1))
             nc.tensor.matmul_mx(
-                out=p_ps[h][:], lhsT=ws_w[:, P * h : P * (h + 1)].bitcast(E4M3), lhsT_scale=ws_s[:, P * h : P * (h + 1)],
+                out=p_ps[h][:], lhsT=ws_w[:, features].bitcast(E4M3), lhsT_scale=ws_s[:, features],
                 rhs=sx_w[:].bitcast(E4M3), rhs_scale=sx_s, start=True, stop=False,
             )
 
-        a_sb = [sb.tile([P, 2, J], F32, name="a_sb%d" % u) for u in range(2)]
-        b_sb = [sb.tile([P, 2, J], F32, name="b_sb%d" % u) for u in range(2)]
-        ga = sb.tile([P, 4, O], F32, name="ga")
-        gb = sb.tile([P, 4, O], F32, name="gb")
+        a_sb = [sb.tile([P, 2, J], F32, name="a_sb%d" % u) for u in HALVES]
+        b_sb = [sb.tile([P, 2, J], F32, name="b_sb%d" % u) for u in HALVES]
+        a_picked = sb.tile([P, PACK, O], F32, name="a_picked")
+        b_picked = sb.tile([P, PACK, O], F32, name="b_picked")
 
-        def pick_v(dst, src, lst, t):
-            nc.vector.tensor_copy(dst[:, t, :], src[t // 2][:, t % 2, :].indirect(lst[:]))
+        def pick_on_vector(dst, src, entries, t):
+            nc.vector.tensor_copy(dst[:, t, :], src[t // 2][:, t % 2, :].indirect(entries[:]))
 
-        def pick_s(dst, src, lst, t):
-            nc.scalar.activation(dst[:, t, :], src[t // 2][:, t % 2, :].indirect(lst[:]), COPY)
+        def pick_on_scalar(dst, src, entries, t):
+            nc.scalar.activation(dst[:, t, :], src[t // 2][:, t % 2, :].indirect(entries[:]), COPY)
 
-        hid = sb.tile([P, O, 4], BF16, name="hid", align_bytes=64)
+        hid = sb.tile([P, O, PACK], BF16, name="hid", align_bytes=64)
 
-        def larger(u):
-            nc.vector.tensor_tensor(
-                out=hid[:, :, 2 * u : 2 * u + 2],
-                in0=ga[:, 2 * u : 2 * u + 2, :].rearrange("p t o -> p o t"),
-                in1=gb[:, 2 * u : 2 * u + 2, :].rearrange("p t o -> p o t"),
-                op=MAX,
-            )
-
-        nc.scalar.activation(a_sb[0][:], a_ps[0][:], COPY)
-        nc.scalar.activation(a_sb[1][:], a_ps[1][:], COPY)
-        pick_v(ga, a_sb, l3, 0)
-        pick_v(ga, a_sb, l3, 1)
-        pick_s(ga, a_sb, l3, 2)
-        pick_s(ga, a_sb, l3, 3)
-        for u in range(2):
+        for u in HALVES:
+            nc.scalar.activation(a_sb[u][:], a_ps[u][:], COPY)
+        for t in range(2):
+            pick_on_vector(a_picked, a_sb, idx3, t)
+        for t in range(2, PACK):
+            pick_on_scalar(a_picked, a_sb, idx3, t)
+        for u in HALVES:
             nc.vector.tensor_copy(b_sb[u][:, 0, :], b_ps[2 * u][:])
             nc.scalar.activation(b_sb[u][:, 1, :], b_ps[2 * u + 1][:], COPY)
-        for u in range(2):
-            pick_v(gb, b_sb, l4, 2 * u)
-            pick_s(gb, b_sb, l4, 2 * u + 1)
-        larger(0)
-        larger(1)
-        hq_w = sb.tile([P, O], U32, name="hq_w", align_bytes=64)
-        hq_s = sb.tile([P, O], U8, name="hq_s", align_bytes=64)
-        nc.vector.quantize_mx(out=hq_w[:].bitcast(E5M2), scales=hq_s[:], in_=hid[:].rearrange("p o t -> p (o t)"))
+        for u in HALVES:
+            pick_on_vector(b_picked, b_sb, idx4, 2 * u)
+            pick_on_scalar(b_picked, b_sb, idx4, 2 * u + 1)
 
-        for h in range(2):
+        for u in HALVES:
+            pair = slice(2 * u, 2 * u + 2)
+            nc.vector.tensor_tensor(
+                out=hid[:, :, pair],
+                in0=a_picked[:, pair, :].rearrange("p t o -> p o t"),
+                in1=b_picked[:, pair, :].rearrange("p t o -> p o t"),
+                op=MAX,
+            )
+        hid_w = sb.tile([P, O], U32, name="hid_w", align_bytes=64)
+        hid_s = sb.tile([P, O], U8, name="hid_s", align_bytes=64)
+        nc.vector.quantize_mx(out=hid_w[:].bitcast(E5M2), scales=hid_s[:], in_=hid[:].rearrange("p o t -> p (o t)"))
+
+        for h in HALVES:
             nc.tensor.matmul_mx(
-                out=p_ps[h][:], lhsT=wb_w[:, 2 * P * h : 2 * P * (h + 1)].bitcast(E2M1), lhsT_scale=wb_s[:, P * h : P * (h + 1)],
-                rhs=hq_w[:].bitcast(E5M2), rhs_scale=hq_s[:], start=False, stop=True,
+                out=p_ps[h][:], lhsT=wb_w[:, 2 * P * h : 2 * P * (h + 1)].bitcast(E2M1),
+                lhsT_scale=wb_s[:, P * h : P * (h + 1)],
+                rhs=hid_w[:].bitcast(E5M2), rhs_scale=hid_s[:], start=False, stop=True,
             )
 
-        p_sb = [sb.tile([P, O], F32, name="p_sb%d" % h) for h in range(2)]
+        p_sb = [sb.tile([P, O], F32, name="p_sb%d" % h) for h in HALVES]
         nc.vector.tensor_copy(p_sb[0][:], p_ps[0][:])
-        nc.vector.tensor_copy(pages[0][:].indirect(l5[:]), p_sb[0][:])
+        nc.vector.tensor_copy(pages[0][:].indirect(idx5[:]), p_sb[0][:])
         nc.sync.dma_start(out=out[0:P, :], in_=pages[0][:])
         nc.scalar.activation(p_sb[1][:], p_ps[1][:], COPY)
-        nc.scalar.activation(pages[1][:].indirect(l5[:]), p_sb[1][:], COPY)
+        nc.scalar.activation(pages[1][:].indirect(idx5[:]), p_sb[1][:], COPY)
         nc.scalar.dma_start(out=out[P : 2 * P, :], in_=pages[1][:])

from contextlib import ExitStack

import concourse.mybir as mybir

FLOPS = 335544320

F32 = mybir.dt.float32
BF16 = mybir.dt.bfloat16
I32 = mybir.dt.int32
U32 = mybir.dt.uint32
U16 = mybir.dt.uint16
U8 = mybir.dt.uint8
E4M3 = mybir.dt.float8_e4m3fn_x4
E5M2 = mybir.dt.float8_e5m2_x4
E2M1 = mybir.dt.float4_e2m1fn_x4
COPY = mybir.ActivationFunctionType.Copy
MAX = mybir.AluOpType.max

P = 128
PACK = 4
QUADRANT = 32
BLOCKS = 16
LIST_ROWS = 16
T = 1024
J = 256
R = 512
O = 128
N = 256
E = 1024
HALVES = range(2)


def load_scale_rows(nc, scale_tile, rows):
    per_quadrant = BLOCKS * QUADRANT // P
    for i in range(per_quadrant):
        nc.sync.dma_start(
            out=scale_tile[i:P:QUADRANT, :].bitcast(I32), in_=rows[0, i:BLOCKS:per_quadrant, :].bitcast(I32)
        )


def load_bytes(nc, tile, packed):
    nc.sync.dma_start(out=tile[:].bitcast(I32), in_=packed.bitcast(I32))


def e4m3_rows(words):
    return words[0].rearrange("p c t -> p (c t)")


def tile_list_oneforboth_looked_skip_scattered_kernel(
    tc, xt_words, xt_scales, xo_words, xo_scales, w_words, w_scales, wb_words, wb_scales,
    sx_words, sx_scales, ws_words, ws_scales, offs, offs2, offs3, offs4, offs5, out,
):
    nc = tc.nc
    with ExitStack() as ctx:
        sb = ctx.enter_context(tc.tile_pool(name="sb", bufs=1))
        ps = ctx.enter_context(tc.psum_pool(name="ps", bufs=1))

        idx = sb.tile([P, J // LIST_ROWS], U16, name="idx")
        idx2 = sb.tile([P, J // LIST_ROWS], U16, name="idx2")
        idx3 = sb.tile([P, O // LIST_ROWS], U16, name="idx3")
        idx4 = sb.tile([P, O // LIST_ROWS], U16, name="idx4")
        idx5 = sb.tile([P, O // LIST_ROWS], U16, name="idx5")
        xt_w = sb.tile([P, T], U16, name="xt_w", align_bytes=64)
        xt_s = sb.tile([P, T], U8, name="xt_s", align_bytes=64)
        xo_w = sb.tile([P, T], U32, name="xo_w", align_bytes=64)
        xo_s = sb.tile([P, T], U8, name="xo_s", align_bytes=64)
        w_w = sb.tile([P, R], U32, name="w_w", align_bytes=64)
        w_s = sb.tile([P, R], U8, name="w_s", align_bytes=64)
        wb_w = sb.tile([P, 2 * N], U8, name="wb_w", align_bytes=64)
        ws_w = sb.tile([P, N], U32, name="ws_w", align_bytes=64)
        sx_w = sb.tile([P, O], U32, name="sx_w", align_bytes=64)
        stage2_s = sb.tile([P, 2 * N + O], U8, name="stage2_s", align_bytes=64)
        wb_s = stage2_s[:, 0:N]
        ws_s = stage2_s[:, N : 2 * N]
        sx_s = stage2_s[:, 2 * N : 2 * N + O]
        pages = [sb.tile([P, E], F32, name="page%d" % h) for h in HALVES]

        for scale_tile in (xt_s, w_s, xo_s, stage2_s):
            nc.vector.memset(scale_tile[:].bitcast(I32), 0)
        for h in HALVES:
            nc.vector.memset(pages[h][:], 0.0)

        nc.sync.dma_start(idx[:], offs)
        nc.sync.dma_start(idx2[:], offs2)
        load_scale_rows(nc, xt_s, xt_scales)
        load_bytes(nc, xt_w, xt_words[0])
        load_bytes(nc, w_w, e4m3_rows(w_words))
        load_scale_rows(nc, w_s, w_scales)
        load_bytes(nc, xo_w, e4m3_rows(xo_words))
        load_scale_rows(nc, xo_s, xo_scales)
        nc.sync.dma_start(idx3[:], offs3)
        load_bytes(nc, ws_w, e4m3_rows(ws_words))
        load_bytes(nc, sx_w, e4m3_rows(sx_words))
        nc.sync.dma_start(idx4[:], offs4)
        load_scale_rows(nc, ws_s, ws_scales)
        load_scale_rows(nc, sx_s, sx_scales)
        load_bytes(nc, wb_w, wb_words[0])
        load_scale_rows(nc, wb_s, wb_scales)
        nc.sync.dma_start(idx5[:], offs5)

        xt_picked_w = sb.tile([P, J], U16, name="xt_picked_w", align_bytes=64)
        xt_picked_s = sb.tile([P, J], U8, name="xt_picked_s", align_bytes=64)
        xo_picked_w = sb.tile([P, J], U32, name="xo_picked_w", align_bytes=64)
        xo_picked_s = sb.tile([P, J], U8, name="xo_picked_s", align_bytes=64)
        dealt_w = [sb.tile([P, 2, P], U32, name="dealt_w%d" % u, align_bytes=64) for u in HALVES]
        dealt_s = [sb.tile([P, 2, P], U8, name="dealt_s%d" % u, align_bytes=64) for u in HALVES]

        nc.vector.tensor_copy(xt_picked_s[:], xt_s[:].indirect(idx[:]))
        nc.vector.tensor_copy(xt_picked_w[:], xt_w[:].indirect(idx[:]))
        for u in HALVES:
            pair = slice(2 * u, 2 * u + 2)
            nc.scalar.copy(
                out=dealt_w[u][:].rearrange("p t q -> p q t"),
                in_=w_w[:].rearrange("p (q t) -> p q t", t=PACK)[:, :, pair],
            )
            nc.vector.tensor_copy(out=dealt_s[u][:], in_=w_s[:].rearrange("p (q t) -> p t q", t=PACK)[:, pair, :])
        nc.vector.tensor_copy(xo_picked_w[:], xo_w[:].indirect(idx2[:]))
        half_list = P // LIST_ROWS
        for g in HALVES:
            nc.vector.tensor_copy(
                xo_picked_s[:, P * g : P * (g + 1)], xo_s[:].indirect(idx2[:, half_list * g : half_list * (g + 1)])
            )

        a_ps = [ps.tile([P, 2, J], F32, name="a_ps%d" % u) for u in HALVES]
        b_ps = [ps.tile([P, J], F32, name="b_ps%d" % t) for t in range(PACK)]

        def first_stage(dst, t, words, scales):
            nc.tensor.matmul_mx(
                out=dst, lhsT=dealt_w[t // 2][:, t % 2, :].bitcast(E4M3), lhsT_scale=dealt_s[t // 2][:, t % 2, :],
                rhs=words, rhs_scale=scales, start=True, stop=True,
            )

        for t in range(PACK):
            first_stage(a_ps[t // 2][:, t % 2, :], t, xt_picked_w[:].bitcast(E2M1), xt_picked_s[:])
        for g in HALVES:
            slots = slice(P * g, P * (g + 1))
            for t in range(2):
                first_stage(b_ps[t][:, slots], t, xo_picked_w[:, slots].bitcast(E4M3), xo_picked_s[:, slots])
        for t in range(2, PACK):
            first_stage(b_ps[t][:], t, xo_picked_w[:].bitcast(E4M3), xo_picked_s[:])

        p_ps = [ps.tile([P, O], F32, name="p_ps%d" % h) for h in HALVES]
        for h in HALVES:
            features = slice(P * h, P * (h + 1))
            nc.tensor.matmul_mx(
                out=p_ps[h][:], lhsT=ws_w[:, features].bitcast(E4M3), lhsT_scale=ws_s[:, features],
                rhs=sx_w[:].bitcast(E4M3), rhs_scale=sx_s, start=True, stop=False,
            )

        a_sb = [sb.tile([P, 2, J], F32, name="a_sb%d" % u) for u in HALVES]
        b_sb = [sb.tile([P, 2, J], F32, name="b_sb%d" % u) for u in HALVES]
        a_picked = sb.tile([P, PACK, O], F32, name="a_picked")
        b_picked = sb.tile([P, PACK, O], F32, name="b_picked")

        def pick_on_vector(dst, src, entries, t):
            nc.vector.tensor_copy(dst[:, t, :], src[t // 2][:, t % 2, :].indirect(entries[:]))

        def pick_on_scalar(dst, src, entries, t):
            nc.scalar.activation(dst[:, t, :], src[t // 2][:, t % 2, :].indirect(entries[:]), COPY)

        hid = sb.tile([P, O, PACK], BF16, name="hid", align_bytes=64)

        for u in HALVES:
            nc.scalar.activation(a_sb[u][:], a_ps[u][:], COPY)
        for t in range(2):
            pick_on_vector(a_picked, a_sb, idx3, t)
        for t in range(2, PACK):
            pick_on_scalar(a_picked, a_sb, idx3, t)
        for u in HALVES:
            nc.vector.tensor_copy(b_sb[u][:, 0, :], b_ps[2 * u][:])
            nc.scalar.activation(b_sb[u][:, 1, :], b_ps[2 * u + 1][:], COPY)
        for u in HALVES:
            pick_on_vector(b_picked, b_sb, idx4, 2 * u)
            pick_on_scalar(b_picked, b_sb, idx4, 2 * u + 1)

        for u in HALVES:
            pair = slice(2 * u, 2 * u + 2)
            nc.vector.tensor_tensor(
                out=hid[:, :, pair],
                in0=a_picked[:, pair, :].rearrange("p t o -> p o t"),
                in1=b_picked[:, pair, :].rearrange("p t o -> p o t"),
                op=MAX,
            )
        hid_w = sb.tile([P, O], U32, name="hid_w", align_bytes=64)
        hid_s = sb.tile([P, O], U8, name="hid_s", align_bytes=64)
        nc.vector.quantize_mx(out=hid_w[:].bitcast(E5M2), scales=hid_s[:], in_=hid[:].rearrange("p o t -> p (o t)"))

        for h in HALVES:
            nc.tensor.matmul_mx(
                out=p_ps[h][:], lhsT=wb_w[:, 2 * P * h : 2 * P * (h + 1)].bitcast(E2M1),
                lhsT_scale=wb_s[:, P * h : P * (h + 1)],
                rhs=hid_w[:].bitcast(E5M2), rhs_scale=hid_s[:], start=False, stop=True,
            )

        p_sb = [sb.tile([P, O], F32, name="p_sb%d" % h) for h in HALVES]
        nc.vector.tensor_copy(p_sb[0][:], p_ps[0][:])
        nc.vector.tensor_copy(pages[0][:].indirect(idx5[:]), p_sb[0][:])
        nc.sync.dma_start(out=out[0:P, :], in_=pages[0][:])
        nc.scalar.activation(p_sb[1][:], p_ps[1][:], COPY)
        nc.scalar.activation(pages[1][:].indirect(idx5[:]), p_sb[1][:], COPY)
        nc.scalar.dma_start(out=out[P : 2 * P, :], in_=pages[1][:])
